import numpy as np
import ml_dtypes


def mxq(x, axis, fmt="e4m3"):
    dtype, down = {"e4m3": (ml_dtypes.float8_e4m3fn, 7), "e5m2": (ml_dtypes.float8_e5m2, 14)}[fmt]
    v = np.moveaxis(np.asarray(x, np.float32).astype(ml_dtypes.bfloat16).astype(np.float64), axis, -1)
    blocks = v.reshape(v.shape[:-1] + (-1, 32))
    amax = np.abs(blocks).max(-1, keepdims=True)
    byte = np.maximum(np.where(amax > 0, np.frexp(amax)[1] - 1 + 127, 0) - down, 1)
    scale = np.exp2(byte - 127.0)
    codes = (blocks / scale).astype(np.float32).astype(dtype).astype(np.float64)
    return np.moveaxis((codes * scale).reshape(v.shape), -1, axis)


WIDE = False


def mx_kscale(k):
    if not WIDE:
        return np.ones(k)
    levels = np.array([10, -10, 5, -5, 0])
    if k % 512:
        return np.exp2(np.random.permutation(np.resize(levels, k // 32))).repeat(32)
    a = np.empty((k // 512, 16))
    for p in range(k // 512):
        a[p, :8] = np.random.permutation(np.resize(levels, 8))
        for g in range(8):
            far = levels[np.abs(levels - a[p, g]) >= 10]
            a[p, g + 8] = far[np.random.randint(len(far))]
    return np.exp2(a.ravel()).repeat(32)


def f64(x):
    return np.asarray(x).astype(np.float64)


def striped(idx):
    return np.tile(np.asarray(idx).reshape(-1, 16).T, (8, 1)).astype(np.uint16)


def unstriped(offs):
    return offs[:16].T.reshape(-1).astype(np.int64)


E2M1 = np.array([0.0, 0.5, 1.0, 1.5, 2.0, 3.0, 4.0, 6.0, -0.0, -0.5, -1.0, -1.5, -2.0, -3.0, -4.0, -6.0])


def pack_weight(w, fmt):
    k, n = w.shape
    w = f64(np.asarray(w, np.float32).astype(ml_dtypes.bfloat16)).reshape(k // 32, 32, n)
    amax = np.abs(w).max(1)
    if fmt == "e4m3":
        byte = np.frexp(amax)[1] - 1 + 127 - 7
    else:
        mant, ex = np.frexp(amax / 6.0)
        byte = np.where(mant > 0.5, ex, ex - 1) + 127
    byte = np.clip(np.where(amax > 0, byte, 1), 1, 254)
    scaled = (w * np.exp2(127.0 - byte)[:, None, :]).reshape(k, n).astype(np.float32)
    by_word = np.ascontiguousarray(scaled.reshape(k // 512, 128, 4, n).transpose(0, 1, 3, 2))
    if fmt == "e4m3":
        words = by_word.astype(ml_dtypes.float8_e4m3fn).view(np.uint8)
    else:
        c = by_word.astype(ml_dtypes.float4_e2m1fn).view(np.uint8) & 0xF
        words = (c[..., 0::2] | (c[..., 1::2] << 4)).reshape(k // 512, 128, 2 * n)
    return np.ascontiguousarray(words), np.ascontiguousarray(byte.astype(np.uint8).reshape(k // 512, 16, n))


def unpack_weight(words, scales, fmt):
    g, _, n = scales.shape
    words = np.ascontiguousarray(words).reshape(g, 128, n, -1)
    if fmt == "e4m3":
        vals = words.view(ml_dtypes.float8_e4m3fn).astype(np.float64)
    else:
        nib = np.empty((g, 128, n, 4), np.uint8)
        nib[..., 0::2] = words & 0xF
        nib[..., 1::2] = words >> 4
        vals = E2M1[nib]
    vals = vals * np.repeat(np.exp2(scales.astype(np.float64) - 127.0), 8, axis=1)[..., None]
    return vals.transpose(0, 1, 3, 2).reshape(g * 512, n)


def sigmoid(v):
    return 1.0 / (1.0 + np.exp(-v))


B, N, T, D, NQ = 1, 512, 2048, 512, 256


def setup_inputs():
    n = np.random.standard_normal
    idx = np.random.permutation(T)[:B * N]
    s = mx_kscale(D)[:, None]
    kp = pack_weight(n((D, T)) / s, "e4m3")
    cp = pack_weight(n((D, T)) / s, "e4m3")
    return {
        "qT": (n((B, D, NQ)) * s * (1.00 / np.sqrt(D))).astype(np.float32),
        "k_words": kp[0],
        "k_scales": kp[1],
        "c_words": cp[0],
        "c_scales": cp[1],
        "offs": striped(idx),
    }


def reference(qT, k_words, k_scales, c_words, c_scales, offs):
    idx = unstriped(offs)
    pick = lambda x, which: x[:, which].reshape(x.shape[0], B, -1).transpose(1, 0, 2)
    k = unpack_weight(k_words, k_scales, "e4m3")
    kg = pick(k, idx)
    c = unpack_weight(c_words, c_scales, "e4m3")
    cg = pick(c, idx)
    qq = mxq(f64(qT), 1, "e4m3")
    a = qq.transpose(0, 2, 1) @ kg
    z = qq.transpose(0, 2, 1) @ cg
    y = sigmoid(a) * sigmoid(z)
    return y

@@ -1,0 +1,116 @@
+from contextlib import ExitStack
+
+import concourse.mybir as mybir
+
+D, T, N, NQ = 512, 2048, 512, 256
+FLOPS = 2 * 2 * NQ * N * D
+
+F32 = mybir.dt.float32
+BF16 = mybir.dt.bfloat16
+I32 = mybir.dt.int32
+U32 = mybir.dt.uint32
+U16 = mybir.dt.uint16
+U8 = mybir.dt.uint8
+FP8X4 = mybir.dt.float8_e4m3fn_x4
+SIGMOID = mybir.ActivationFunctionType.Sigmoid
+MULT = mybir.AluOpType.mult
+
+P = 128
+PACK = 4
+HALF = N // 2
+Q_TILES = NQ // P
+ROW_STEP = 8
+PLANE_ROW = 4
+
+
+def tile_attend_both_and_topk_kernel(tc, qT, k_words, k_scales, c_words, c_scales, offs, out):
+    nc = tc.nc
+    with ExitStack() as ctx:
+        held = ctx.enter_context(tc.tile_pool(name="held", bufs=1))
+        psum = ctx.enter_context(tc.psum_pool(name="psum", bufs=1))
+
+        q_raw = held.tile([P, PACK, NQ], F32, name="q_raw")
+        q_rows = qT[0].rearrange("(p j) w -> p j w", j=PACK)
+        nc.sync.dma_start(q_raw[:, 0:2, :], q_rows[:, 0:2, :])
+        offsets = held.tile([P, N // 16], U16, name="offsets")
+        nc.sync.dma_start(offsets[:], offs)
+        scale_pools = []
+        for s, (name, scales) in enumerate((("k", k_scales), ("c", c_scales))):
+            pool_tile = held.tile([P, T], U8, name=name + "_scale_pool", align_bytes=64)
+            nc.vector.memset(pool_tile[:].bitcast(I32), 0)
+            nc.sync.dma_start(pool_tile[:].bitcast(I32)[PLANE_ROW * s : P : ROW_STEP, :], scales[0].bitcast(I32))
+            scale_pools.append(pool_tile)
+
+        nc.sync.dma_start(q_raw[:, 2:4, :], q_rows[:, 2:4, :])
+        word_pools = []
+        for name, words in (("k", k_words), ("c", c_words)):
+            pool_tile = held.tile([P, T], I32, name=name + "_word_pool", align_bytes=64)
+            nc.sync.dma_start(pool_tile[:], words[0].rearrange("p n t -> p (n t)").bitcast(I32))
+            word_pools.append(pool_tile)
+
+        warm_in = held.tile([P, 1], F32, name="warm_in")
+        warm_out = held.tile([P, 1], F32, name="warm_out")
+        nc.gpsimd.memset(warm_in[:], 0.0)
+        nc.scalar.activation(warm_out[:], warm_in[:], SIGMOID)
+
+        planes = []
+        for s, name in enumerate("kc"):
+            picked = held.tile([P, N], U8, name=name + "_scales_picked", align_bytes=64)
+            nc.vector.tensor_copy(picked[:], scale_pools[s][:].indirect(offsets[:]))
+            plane = held.tile([P, N], U8, name=name + "_plane", align_bytes=64)
+            plane_w = plane[:].bitcast(I32)
+            first_row = PLANE_ROW * s
+            nc.vector.tensor_copy(plane_w, picked[:].bitcast(I32))
+            for r in range(1, 4):
+                nc.scalar.dma_start(plane_w[first_row + r : P : 32, :], plane_w[first_row + ROW_STEP * r : P : 32, :])
+            planes.append(plane)
+
+        q_grouped = held.tile([P, NQ, PACK], BF16, name="q_grouped", align_bytes=64)
+        nc.scalar.copy(
+            q_grouped[:].rearrange("p (c i) t -> p c t i", i=4),
+            q_raw[:].rearrange("p t (c i) -> p c t i", i=4),
+        )
+        q_codes = held.tile([P, NQ], U32, name="q_codes", align_bytes=64)
+        q_scales = held.tile([P, NQ], U8, name="q_scales", align_bytes=64)
+        nc.vector.quantize_mx(
+            out=q_codes[:].bitcast(FP8X4), scales=q_scales[:], in_=q_grouped[:].rearrange("p w t -> p (w t)")
+        )
+
+        def gather_words(s, h):
+            picked = held.tile([P, HALF], U32, name="words_%d_%d" % (s, h), align_bytes=64)
+            cols = slice(h * HALF // 16, (h + 1) * HALF // 16)
+            nc.vector.tensor_copy(picked[:], word_pools[s][:].bitcast(U32).indirect(offsets[:, cols]))
+            return picked
+
+        def score(dst, s, h, t, picked):
+            q_cols = slice(t * P, (t + 1) * P)
+            nc.tensor.matmul_mx(
+                out=dst,
+                lhsT=q_codes[:, q_cols].bitcast(FP8X4),
+                lhsT_scale=q_scales[:, q_cols],
+                rhs=picked[:].bitcast(FP8X4),
+                rhs_scale=planes[s][PLANE_ROW * s : P, h * HALF : (h + 1) * HALF],
+                start=True,
+                stop=True,
+            )
+
+        first = []
+        for h in range(2):
+            picked = gather_words(0, h)
+            bank = psum.tile([P, Q_TILES, HALF], F32, name="a_bank_%d" % h)
+            for t in range(Q_TILES):
+                score(bank[:, t, :], 0, h, t, picked)
+            sig = held.tile([P, Q_TILES, HALF], F32, name="a_sig_%d" % h)
+            nc.scalar.activation(sig[:], bank[:], SIGMOID)
+            first.append(sig)
+
+        second_words = [gather_words(1, h) for h in range(2)]
+        for h in range(2):
+            for t in range(Q_TILES):
+                bank = psum.tile([P, HALF], F32, name="z_bank_%d_%d" % (h, t))
+                score(bank[:], 1, h, t, second_words[h])
+                sig = held.tile([P, HALF], F32, name="z_sig_%d_%d" % (h, t))
+                nc.scalar.activation(sig[:], bank[:], SIGMOID)
+                y = held.tile([P, HALF], F32, name="y_%d_%d" % (h, t))
+                nc.vector.tensor_tensor(y[:], first[h][:, t, :], sig[:], MULT)
+                nc.sync.dma_start(out[0, t * P : (t + 1) * P, h * HALF : (h + 1) * HALF], y[:])

@@ -43,9 +43,9 @@ def tile_attend_both_and_topk_kernel(tc, qT, k_words, k_scales, c_words, c_scale
 
         nc.sync.dma_start(q_raw[:, 2:4, :], q_rows[:, 2:4, :])
         word_pools = []
-        for name, words in (("k", k_words), ("c", c_words)):
+        for name, words, piece in (("k", k_words, 8192), ("c", c_words, 4096)):
             pool_tile = held.tile([P, T], I32, name=name + "_word_pool", align_bytes=64)
-            nc.sync.dma_start(pool_tile[:], words[0].rearrange("p n t -> p (n t)").bitcast(I32))
+            nc.sync.dma_start(pool_tile[:], words[0].rearrange("p n t -> p (n t)").bitcast(I32), max_dma_last_dim=piece)
             word_pools.append(pool_tile)
 
         warm_in = held.tile([P, 1], F32, name="warm_in")
@@ -55,7 +55,7 @@ def tile_attend_both_and_topk_kernel(tc, qT, k_words, k_scales, c_words, c_scale
 
         planes = []
         for s, name in enumerate("kc"):
-            picked = held.tile([P, N], U8, name=name + "_scales_picked", align_bytes=64)
+            picked = held.tile([P, N], U8, name=name + "_scales_picked", tag=name + "_staging", align_bytes=64)
             nc.vector.tensor_copy(picked[:], scale_pools[s][:].indirect(offsets[:]))
             plane = held.tile([P, N], U8, name=name + "_plane", align_bytes=64)
             plane_w = plane[:].bitcast(I32)
@@ -65,16 +65,21 @@ def tile_attend_both_and_topk_kernel(tc, qT, k_words, k_scales, c_words, c_scale
                 nc.scalar.dma_start(plane_w[first_row + r : P : 32, :], plane_w[first_row + ROW_STEP * r : P : 32, :])
             planes.append(plane)
 
-        q_grouped = held.tile([P, NQ, PACK], BF16, name="q_grouped", align_bytes=64)
-        nc.scalar.copy(
-            q_grouped[:].rearrange("p (c i) t -> p c t i", i=4),
-            q_raw[:].rearrange("p t (c i) -> p c t i", i=4),
-        )
-        q_codes = held.tile([P, NQ], U32, name="q_codes", align_bytes=64)
-        q_scales = held.tile([P, NQ], U8, name="q_scales", align_bytes=64)
-        nc.vector.quantize_mx(
-            out=q_codes[:].bitcast(FP8X4), scales=q_scales[:], in_=q_grouped[:].rearrange("p w t -> p (w t)")
-        )
+        q_codes = []
+        q_scales = []
+        for t in range(Q_TILES):
+            grouped = held.tile([P, P, PACK], BF16, name="q_grouped_%d" % t, tag=("q_staging", "k_staging")[t], align_bytes=64)
+            nc.scalar.copy(
+                grouped[:].rearrange("p (c i) j -> p c j i", i=4),
+                q_raw[:, :, t * P : (t + 1) * P].rearrange("p j (c i) -> p c j i", i=4),
+            )
+            codes = held.tile([P, P], U32, name="q_codes_%d" % t, align_bytes=64)
+            scales = held.tile([P, P], U8, name="q_scales_%d" % t, align_bytes=64)
+            nc.vector.quantize_mx(
+                out=codes[:].bitcast(FP8X4), scales=scales[:], in_=grouped[:].rearrange("p w j -> p (w j)")
+            )
+            q_codes.append(codes)
+            q_scales.append(scales)
 
         def gather_words(s, h):
             picked = held.tile([P, HALF], U32, name="words_%d_%d" % (s, h), align_bytes=64)
@@ -83,34 +88,33 @@ def tile_attend_both_and_topk_kernel(tc, qT, k_words, k_scales, c_words, c_scale
             return picked
 
         def score(dst, s, h, t, picked):
-            q_cols = slice(t * P, (t + 1) * P)
             nc.tensor.matmul_mx(
                 out=dst,
-                lhsT=q_codes[:, q_cols].bitcast(FP8X4),
-                lhsT_scale=q_scales[:, q_cols],
+                lhsT=q_codes[t][:].bitcast(FP8X4),
+                lhsT_scale=q_scales[t][:],
                 rhs=picked[:].bitcast(FP8X4),
                 rhs_scale=planes[s][PLANE_ROW * s : P, h * HALF : (h + 1) * HALF],
                 start=True,
                 stop=True,
             )
 
-        first = []
+        def sigmoid_scores(s, h, t, picked):
+            bank = psum.tile([P, HALF], F32, name="bank_%d_%d_%d" % (s, h, t))
+            score(bank[:], s, h, t, picked)
+            sig = held.tile([P, HALF], F32, name="sig_%d_%d_%d" % (s, h, t))
+            nc.scalar.activation(sig[:], bank[:], SIGMOID)
+            return sig
+
+        first = {}
         for h in range(2):
             picked = gather_words(0, h)
-            bank = psum.tile([P, Q_TILES, HALF], F32, name="a_bank_%d" % h)
             for t in range(Q_TILES):
-                score(bank[:, t, :], 0, h, t, picked)
-            sig = held.tile([P, Q_TILES, HALF], F32, name="a_sig_%d" % h)
-            nc.scalar.activation(sig[:], bank[:], SIGMOID)
-            first.append(sig)
+                first[h, t] = sigmoid_scores(0, h, t, picked)
 
         second_words = [gather_words(1, h) for h in range(2)]
         for h in range(2):
             for t in range(Q_TILES):
-                bank = psum.tile([P, HALF], F32, name="z_bank_%d_%d" % (h, t))
-                score(bank[:], 1, h, t, second_words[h])
-                sig = held.tile([P, HALF], F32, name="z_sig_%d_%d" % (h, t))
-                nc.scalar.activation(sig[:], bank[:], SIGMOID)
+                sig = sigmoid_scores(1, h, t, second_words[h])
                 y = held.tile([P, HALF], F32, name="y_%d_%d" % (h, t))
-                nc.vector.tensor_tensor(y[:], first[h][:, t, :], sig[:], MULT)
+                nc.vector.tensor_tensor(y[:], first[h, t][:], sig[:], MULT)
                 nc.sync.dma_start(out[0, t * P : (t + 1) * P, h * HALF : (h + 1) * HALF], y[:])

@@ -36,7 +36,7 @@ def tile_attend_both_and_topk_kernel(tc, qT, k_words, k_scales, c_words, c_scale
         nc.sync.dma_start(offsets[:], offs)
         scale_pools = []
         for s, (name, scales) in enumerate((("k", k_scales), ("c", c_scales))):
-            pool_tile = held.tile([P, T], U8, name=name + "_scale_pool", align_bytes=64)
+            pool_tile = held.tile([P, T], U8, name=name + "_scale_pool", tag=name + "_scale_pool", align_bytes=64)
             nc.vector.memset(pool_tile[:].bitcast(I32), 0)
             nc.sync.dma_start(pool_tile[:].bitcast(I32)[PLANE_ROW * s : P : ROW_STEP, :], scales[0].bitcast(I32))
             scale_pools.append(pool_tile)
@@ -55,31 +55,34 @@ def tile_attend_both_and_topk_kernel(tc, qT, k_words, k_scales, c_words, c_scale
 
         planes = []
         for s, name in enumerate("kc"):
-            picked = held.tile([P, N], U8, name=name + "_scales_picked", tag=name + "_staging", align_bytes=64)
-            nc.vector.tensor_copy(picked[:], scale_pools[s][:].indirect(offsets[:]))
             plane = held.tile([P, N], U8, name=name + "_plane", align_bytes=64)
             plane_w = plane[:].bitcast(I32)
+            if s == 0:
+                nc.vector.memset(plane_w, 0)
+            picked = held.tile([P, N], U8, name=name + "_scales_picked", tag=name + "_staging", align_bytes=64)
+            picked_w = picked[:].bitcast(I32)
+            nc.vector.tensor_copy(picked[:], scale_pools[s][:].indirect(offsets[:]))
             first_row = PLANE_ROW * s
-            nc.vector.tensor_copy(plane_w, picked[:].bitcast(I32))
-            for r in range(1, 4):
-                nc.scalar.dma_start(plane_w[first_row + r : P : 32, :], plane_w[first_row + ROW_STEP * r : P : 32, :])
+            if s == 1:
+                nc.vector.tensor_copy(plane_w, picked_w)
+            for r in range(s, 4):
+                nc.scalar.dma_start(plane_w[first_row + r : P : 32, :], picked_w[first_row + ROW_STEP * r : P : 32, :])
             planes.append(plane)
 
-        q_codes = []
-        q_scales = []
+        q_codes = held.tile([P, NQ], U32, name="q_codes", tag="c_scale_pool", align_bytes=64)
+        q_scales = held.tile([P, NQ], U8, name="q_scales", align_bytes=64)
         for t in range(Q_TILES):
-            grouped = held.tile([P, P, PACK], BF16, name="q_grouped_%d" % t, tag=("q_staging", "k_staging")[t], align_bytes=64)
+            grouped = held.tile([P, P, PACK], BF16, name="q_grouped_%d" % t, tag=("q_staging", "k_scale_pool")[t], align_bytes=64)
             nc.scalar.copy(
                 grouped[:].rearrange("p (c i) j -> p c j i", i=4),
                 q_raw[:, :, t * P : (t + 1) * P].rearrange("p j (c i) -> p c j i", i=4),
             )
-            codes = held.tile([P, P], U32, name="q_codes_%d" % t, align_bytes=64)
-            scales = held.tile([P, P], U8, name="q_scales_%d" % t, align_bytes=64)
+            q_cols = slice(t * P, (t + 1) * P)
             nc.vector.quantize_mx(
-                out=codes[:].bitcast(FP8X4), scales=scales[:], in_=grouped[:].rearrange("p w j -> p (w j)")
+                out=q_codes[:, q_cols].bitcast(FP8X4),
+                scales=q_scales[:, q_cols],
+                in_=grouped[:].rearrange("p w j -> p (w j)"),
             )
-            q_codes.append(codes)
-            q_scales.append(scales)
 
         def gather_words(s, h):
             picked = held.tile([P, HALF], U32, name="words_%d_%d" % (s, h), align_bytes=64)
@@ -90,8 +93,8 @@ def tile_attend_both_and_topk_kernel(tc, qT, k_words, k_scales, c_words, c_scale
         def score(dst, s, h, t, picked):
             nc.tensor.matmul_mx(
                 out=dst,
-                lhsT=q_codes[t][:].bitcast(FP8X4),
-                lhsT_scale=q_scales[t][:],
+                lhsT=q_codes[:, t * P : (t + 1) * P].bitcast(FP8X4),
+                lhsT_scale=q_scales[:, t * P : (t + 1) * P],
                 rhs=picked[:].bitcast(FP8X4),
                 rhs_scale=planes[s][PLANE_ROW * s : P, h * HALF : (h + 1) * HALF],
                 start=True,

@@ -31,7 +31,7 @@ def tile_attend_both_and_topk_kernel(tc, qT, k_words, k_scales, c_words, c_scale
 
         q_raw = held.tile([P, PACK, NQ], F32, name="q_raw")
         q_rows = qT[0].rearrange("(p j) w -> p j w", j=PACK)
-        nc.sync.dma_start(q_raw[:, 0:2, :], q_rows[:, 0:2, :])
+        nc.sync.dma_start(q_raw[:, 0:3, :], q_rows[:, 0:3, :])
         offsets = held.tile([P, N // 16], U16, name="offsets")
         nc.sync.dma_start(offsets[:], offs)
         scale_pools = []
@@ -40,8 +40,9 @@ def tile_attend_both_and_topk_kernel(tc, qT, k_words, k_scales, c_words, c_scale
             nc.vector.memset(pool_tile[:].bitcast(I32), 0)
             nc.sync.dma_start(pool_tile[:].bitcast(I32)[PLANE_ROW * s : P : ROW_STEP, :], scales[0].bitcast(I32))
             scale_pools.append(pool_tile)
+            if s == 0:
+                nc.sync.dma_start(q_raw[:, 3, :], q_rows[:, 3, :])
 
-        nc.sync.dma_start(q_raw[:, 2:4, :], q_rows[:, 2:4, :])
         word_pools = []
         for name, words, piece in (("k", k_words, 8192), ("c", c_words, 4096)):
             pool_tile = held.tile([P, T], I32, name=name + "_word_pool", align_bytes=64)

from contextlib import ExitStack

import concourse.mybir as mybir

D, T, N, NQ = 512, 2048, 512, 256
FLOPS = 2 * 2 * NQ * N * D

F32 = mybir.dt.float32
BF16 = mybir.dt.bfloat16
I32 = mybir.dt.int32
U32 = mybir.dt.uint32
U16 = mybir.dt.uint16
U8 = mybir.dt.uint8
FP8X4 = mybir.dt.float8_e4m3fn_x4
SIGMOID = mybir.ActivationFunctionType.Sigmoid
MULT = mybir.AluOpType.mult

P = 128
PACK = 4
HALF = N // 2
Q_TILES = NQ // P
ROW_STEP = 8
PLANE_ROW = 4


def tile_attend_both_and_topk_kernel(tc, qT, k_words, k_scales, c_words, c_scales, offs, out):
    nc = tc.nc
    with ExitStack() as ctx:
        held = ctx.enter_context(tc.tile_pool(name="held", bufs=1))
        psum = ctx.enter_context(tc.psum_pool(name="psum", bufs=1))

        q_raw = held.tile([P, PACK, NQ], F32, name="q_raw")
        q_rows = qT[0].rearrange("(p j) w -> p j w", j=PACK)
        nc.sync.dma_start(q_raw[:, 0:3, :], q_rows[:, 0:3, :])
        offsets = held.tile([P, N // 16], U16, name="offsets")
        nc.sync.dma_start(offsets[:], offs)
        scale_pools = []
        for s, (name, scales) in enumerate((("k", k_scales), ("c", c_scales))):
            pool_tile = held.tile([P, T], U8, name=name + "_scale_pool", tag=name + "_scale_pool", align_bytes=64)
            nc.vector.memset(pool_tile[:].bitcast(I32), 0)
            nc.sync.dma_start(pool_tile[:].bitcast(I32)[PLANE_ROW * s : P : ROW_STEP, :], scales[0].bitcast(I32))
            scale_pools.append(pool_tile)
            if s == 0:
                nc.sync.dma_start(q_raw[:, 3, :], q_rows[:, 3, :])

        word_pools = []
        for name, words, piece in (("k", k_words, 8192), ("c", c_words, 4096)):
            pool_tile = held.tile([P, T], I32, name=name + "_word_pool", align_bytes=64)
            nc.sync.dma_start(pool_tile[:], words[0].rearrange("p n t -> p (n t)").bitcast(I32), max_dma_last_dim=piece)
            word_pools.append(pool_tile)

        warm_in = held.tile([P, 1], F32, name="warm_in")
        warm_out = held.tile([P, 1], F32, name="warm_out")
        nc.gpsimd.memset(warm_in[:], 0.0)
        nc.scalar.activation(warm_out[:], warm_in[:], SIGMOID)

        planes = []
        for s, name in enumerate("kc"):
            plane = held.tile([P, N], U8, name=name + "_plane", align_bytes=64)
            plane_w = plane[:].bitcast(I32)
            if s == 0:
                nc.vector.memset(plane_w, 0)
            picked = held.tile([P, N], U8, name=name + "_scales_picked", tag=name + "_staging", align_bytes=64)
            picked_w = picked[:].bitcast(I32)
            nc.vector.tensor_copy(picked[:], scale_pools[s][:].indirect(offsets[:]))
            first_row = PLANE_ROW * s
            if s == 1:
                nc.vector.tensor_copy(plane_w, picked_w)
            for r in range(s, 4):
                nc.scalar.dma_start(plane_w[first_row + r : P : 32, :], picked_w[first_row + ROW_STEP * r : P : 32, :])
            planes.append(plane)

        q_codes = held.tile([P, NQ], U32, name="q_codes", tag="c_scale_pool", align_bytes=64)
        q_scales = held.tile([P, NQ], U8, name="q_scales", align_bytes=64)
        for t in range(Q_TILES):
            grouped = held.tile([P, P, PACK], BF16, name="q_grouped_%d" % t, tag=("q_staging", "k_scale_pool")[t], align_bytes=64)
            nc.scalar.copy(
                grouped[:].rearrange("p (c i) j -> p c j i", i=4),
                q_raw[:, :, t * P : (t + 1) * P].rearrange("p j (c i) -> p c j i", i=4),
            )
            q_cols = slice(t * P, (t + 1) * P)
            nc.vector.quantize_mx(
                out=q_codes[:, q_cols].bitcast(FP8X4),
                scales=q_scales[:, q_cols],
                in_=grouped[:].rearrange("p w j -> p (w j)"),
            )

        def gather_words(s, h):
            picked = held.tile([P, HALF], U32, name="words_%d_%d" % (s, h), align_bytes=64)
            cols = slice(h * HALF // 16, (h + 1) * HALF // 16)
            nc.vector.tensor_copy(picked[:], word_pools[s][:].bitcast(U32).indirect(offsets[:, cols]))
            return picked

        def score(dst, s, h, t, picked):
            nc.tensor.matmul_mx(
                out=dst,
                lhsT=q_codes[:, t * P : (t + 1) * P].bitcast(FP8X4),
                lhsT_scale=q_scales[:, t * P : (t + 1) * P],
                rhs=picked[:].bitcast(FP8X4),
                rhs_scale=planes[s][PLANE_ROW * s : P, h * HALF : (h + 1) * HALF],
                start=True,
                stop=True,
            )

        def sigmoid_scores(s, h, t, picked):
            bank = psum.tile([P, HALF], F32, name="bank_%d_%d_%d" % (s, h, t))
            score(bank[:], s, h, t, picked)
            sig = held.tile([P, HALF], F32, name="sig_%d_%d_%d" % (s, h, t))
            nc.scalar.activation(sig[:], bank[:], SIGMOID)
            return sig

        first = {}
        for h in range(2):
            picked = gather_words(0, h)
            for t in range(Q_TILES):
                first[h, t] = sigmoid_scores(0, h, t, picked)

        second_words = [gather_words(1, h) for h in range(2)]
        for h in range(2):
            for t in range(Q_TILES):
                sig = sigmoid_scores(1, h, t, second_words[h])
                y = held.tile([P, HALF], F32, name="y_%d_%d" % (h, t))
                nc.vector.tensor_tensor(y[:], first[h, t][:], sig[:], MULT)
                nc.sync.dma_start(out[0, t * P : (t + 1) * P, h * HALF : (h + 1) * HALF], y[:])
